import numpy as np
import ml_dtypes


def mxq(x, axis, fmt="e4m3"):
    dtype, down = {"e4m3": (ml_dtypes.float8_e4m3fn, 7), "e5m2": (ml_dtypes.float8_e5m2, 14)}[fmt]
    v = np.moveaxis(np.asarray(x, np.float32).astype(ml_dtypes.bfloat16).astype(np.float64), axis, -1)
    blocks = v.reshape(v.shape[:-1] + (-1, 32))
    amax = np.abs(blocks).max(-1, keepdims=True)
    byte = np.maximum(np.where(amax > 0, np.frexp(amax)[1] - 1 + 127, 0) - down, 1)
    scale = np.exp2(byte - 127.0)
    codes = (blocks / scale).astype(np.float32).astype(dtype).astype(np.float64)
    return np.moveaxis((codes * scale).reshape(v.shape), -1, axis)


WIDE = False


def mx_kscale(k):
    if not WIDE:
        return np.ones(k)
    levels = np.array([10, -10, 5, -5, 0])
    if k % 512:
        return np.exp2(np.random.permutation(np.resize(levels, k // 32))).repeat(32)
    a = np.empty((k // 512, 16))
    for p in range(k // 512):
        a[p, :8] = np.random.permutation(np.resize(levels, 8))
        for g in range(8):
            far = levels[np.abs(levels - a[p, g]) >= 10]
            a[p, g + 8] = far[np.random.randint(len(far))]
    return np.exp2(a.ravel()).repeat(32)


def f64(x):
    return np.asarray(x).astype(np.float64)


E2M1 = np.array([0.0, 0.5, 1.0, 1.5, 2.0, 3.0, 4.0, 6.0, -0.0, -0.5, -1.0, -1.5, -2.0, -3.0, -4.0, -6.0])


def pack_weight(w, fmt):
    k, n = w.shape
    w = f64(np.asarray(w, np.float32).astype(ml_dtypes.bfloat16)).reshape(k // 32, 32, n)
    amax = np.abs(w).max(1)
    if fmt == "e4m3":
        byte = np.frexp(amax)[1] - 1 + 127 - 7
    else:
        mant, ex = np.frexp(amax / 6.0)
        byte = np.where(mant > 0.5, ex, ex - 1) + 127
    byte = np.clip(np.where(amax > 0, byte, 1), 1, 254)
    scaled = (w * np.exp2(127.0 - byte)[:, None, :]).reshape(k, n).astype(np.float32)
    by_word = np.ascontiguousarray(scaled.reshape(k // 512, 128, 4, n).transpose(0, 1, 3, 2))
    if fmt == "e4m3":
        words = by_word.astype(ml_dtypes.float8_e4m3fn).view(np.uint8)
    else:
        c = by_word.astype(ml_dtypes.float4_e2m1fn).view(np.uint8) & 0xF
        words = (c[..., 0::2] | (c[..., 1::2] << 4)).reshape(k // 512, 128, 2 * n)
    return np.ascontiguousarray(words), np.ascontiguousarray(byte.astype(np.uint8).reshape(k // 512, 16, n))


def unpack_weight(words, scales, fmt):
    g, _, n = scales.shape
    words = np.ascontiguousarray(words).reshape(g, 128, n, -1)
    if fmt == "e4m3":
        vals = words.view(ml_dtypes.float8_e4m3fn).astype(np.float64)
    else:
        nib = np.empty((g, 128, n, 4), np.uint8)
        nib[..., 0::2] = words & 0xF
        nib[..., 1::2] = words >> 4
        vals = E2M1[nib]
    vals = vals * np.repeat(np.exp2(scales.astype(np.float64) - 127.0), 8, axis=1)[..., None]
    return vals.transpose(0, 1, 3, 2).reshape(g * 512, n)


K, L, T, N = 1024, 512, 512, 512


def setup_inputs():
    n = np.random.standard_normal
    fk = mx_kscale(K)
    fl = mx_kscale(L)
    xtp = pack_weight(n((K, T)) / fk[:, None], "e4m3")
    xqp = pack_weight(n((L, T)) / fl[:, None], "e2m1")
    wsp = pack_weight(n((L, N)) * 1 / np.sqrt(L) * fl[:, None], "e4m3")
    wcp = pack_weight(n((K, N)) * 1 / np.sqrt(K) * fk[:, None], "e2m1")
    return {
        "xt_words": xtp[0],
        "xt_scales": xtp[1],
        "wa": (n((K, N)) * 1 / np.sqrt(K) * fk[:, None]).astype(np.float32),
        "xq_words": xqp[0],
        "xq_scales": xqp[1],
        "ws_words": wsp[0],
        "ws_scales": wsp[1],
        "wc_words": wcp[0],
        "wc_scales": wcp[1],
        "bi": (np.random.uniform(-1.0, 1.0, (1, N))).astype(np.float32),
    }


def reference(xt_words, xt_scales, wa, xq_words, xq_scales, ws_words, ws_scales, wc_words, wc_scales, bi):
    xtu = unpack_weight(xt_words, xt_scales, "e4m3")
    xqu = unpack_weight(xq_words, xq_scales, "e2m1")
    wsu = unpack_weight(ws_words, ws_scales, "e4m3")
    wcu = unpack_weight(wc_words, wc_scales, "e2m1")
    waq = mxq(f64(wa), 0, "e4m3")
    a0 = xtu.T @ waq + xqu.T @ wsu
    b0 = xtu.T @ wcu
    a = a0 + f64(bi)
    b = b0 + f64(bi)
    y = a - b * np.mean(a * b, axis=1, keepdims=True) / (np.mean(np.square(b), axis=1, keepdims=True) + 0.1)
    return y

from contextlib import ExitStack

import concourse.mybir as mybir
from concourse.masks import make_identity

K, L, T, N = 1024, 512, 512, 512
FLOPS = 2 * T * N * (K + L + K)

F32 = mybir.dt.float32
BF16 = mybir.dt.bfloat16
I32 = mybir.dt.int32
U32 = mybir.dt.uint32
U8 = mybir.dt.uint8
FP8X4 = mybir.dt.float8_e4m3fn_x4
FP4X4 = mybir.dt.float4_e2m1fn_x4
ALU = mybir.AluOpType
ACT = mybir.ActivationFunctionType

P = 128
PACK = 4
K_PASS = P * PACK
PASSES = K // K_PASS
TILES = T // P
CHUNKS = N // P
QUADS = 4


def tile_mix_rows_less_common_part_kernel(
    tc, xt_words, xt_scales, wa, xq_words, xq_scales, ws_words, ws_scales, wc_words, wc_scales, bi, out
):
    nc = tc.nc
    with ExitStack() as ctx:
        sb = ctx.enter_context(tc.tile_pool(name="sb", bufs=1))
        ps = ctx.enter_context(tc.psum_pool(name="ps", bufs=1))
        ctx.enter_context(tc.manual_schedule())

        xt = sb.tile([P, PASSES, T], U32, name="xt", align_bytes=64)
        wc = sb.tile([P, PASSES, 2 * N], U8, name="wc", align_bytes=64)
        xq = sb.tile([P, 2 * T], U8, name="xq", align_bytes=64)
        ws = sb.tile([P, N], U32, name="ws", align_bytes=64)
        xt_plane = sb.tile([P, PASSES, T], U8, name="xt_plane", align_bytes=64)
        wc_plane = sb.tile([P, PASSES, N], U8, name="wc_plane", align_bytes=64)
        xq_plane = sb.tile([P, 1, T], U8, name="xq_plane", align_bytes=64)
        ws_plane = sb.tile([P, 1, N], U8, name="ws_plane", align_bytes=64)
        bias_rows = sb.tile([P, P], F32, name="bias_rows")
        bias_col = sb.tile([P, CHUNKS], F32, name="bias_col")
        bias_all = sb.tile([P, N], F32, name="bias_all")
        ident = sb.tile([P, P], F32, name="ident")
        warm = sb.tile([P, 2], F32, name="warm")
        pieces = [(c, z) for c in range(CHUNKS) for z in range(PASSES)]
        raw = {k: sb.tile([P, PACK, P], F32, name="raw%d%d" % k) for k in pieces}
        grouped = {k: sb.tile([P, P, PACK], BF16, name="grouped%d%d" % k, align_bytes=64) for k in pieces}
        wa_codes = {k: sb.tile([P, P], U32, name="wa_codes%d%d" % k, align_bytes=64) for k in pieces}
        wa_plane = {k: sb.tile([P, P], U8, name="wa_plane%d%d" % k, align_bytes=64) for k in pieces}
        b = [sb.tile([P, N], F32, name="b%d" % i) for i in range(TILES)]
        squares = [sb.tile([P, N], F32, name="squares%d" % i) for i in range(TILES)]
        products = [sb.tile([P, N], F32, name="products%d" % i) for i in range(TILES)]
        y = [sb.tile([P, N], F32, name="y%d" % i) for i in range(TILES)]
        a_t = [sb.tile([P, T], F32, name="a_t%d" % c) for c in range(CHUNKS)]
        sum_bb = sb.tile([P, TILES], F32, name="sum_bb")
        neg_den = sb.tile([P, TILES], F32, name="neg_den")
        neg_inv = sb.tile([P, TILES], F32, name="neg_inv")
        sum_ab = sb.tile([P, TILES, 2], F32, name="sum_ab")
        neg_coef = sb.tile([P, TILES], F32, name="neg_coef")

        def load_plane(queue, plane, scales):
            for q in range(QUADS):
                queue.dma_start(
                    out=plane[32 * q : 32 * q + 4, :, :].bitcast(I32),
                    in_=scales[:, 4 * q : 4 * q + 4, :].rearrange("z r n -> r z n").bitcast(I32),
                )

        def load_wa(c, z):
            rows = wa[z * K_PASS : (z + 1) * K_PASS, c * P : (c + 1) * P]
            nc.sync.dma_start(out=raw[c, z][:], in_=rows.rearrange("(p j) n -> p j n", j=PACK))

        for plane in (xt_plane, wc_plane):
            nc.gpsimd.memset(plane[:].bitcast(I32), 0)
        nc.gpsimd.memset(bias_rows[:], 0.0)
        for plane in (ws_plane, xq_plane):
            nc.vector.memset(plane[:].bitcast(I32), 0)
        nc.vector.memset(warm[:], 0.0)
        make_identity(nc, ident[:])

        def load_xt():
            nc.sync.dma_start(out=xt[:].bitcast(I32), in_=xt_words.rearrange("z p n j -> p z (n j)").bitcast(I32))

        def load_wc():
            nc.sync.dma_start(out=wc[:].bitcast(I32), in_=wc_words.rearrange("z p m -> p z m").bitcast(I32))

        def load_xq():
            nc.sync.dma_start(out=xq[:].bitcast(I32), in_=xq_words[0].bitcast(I32))

        def load_ws():
            nc.sync.dma_start(out=ws[:].bitcast(I32), in_=ws_words[0].rearrange("p n j -> p (n j)").bitcast(I32))

        nc.scalar.dma_start(out=bias_rows[0:CHUNKS, :], in_=bi.rearrange("o (c p) -> (o c) p", p=P))
        nc.scalar.activation(out=warm[:, 1:2], in_=warm[:, 0:1], func=ACT.Square)
        load_wa(0, 0)
        load_plane(nc.sync, xt_plane, xt_scales)
        load_xt()
        load_wc()
        load_plane(nc.sync, wc_plane, wc_scales)
        load_plane(nc.gpsimd, ws_plane, ws_scales)
        load_wa(0, 1)
        load_wa(1, 0)
        load_wa(1, 1)
        load_plane(nc.sync, xq_plane, xq_scales)
        load_xq()
        load_ws()
        load_wa(2, 0)
        load_wa(2, 1)
        load_wa(3, 0)
        load_wa(3, 1)

        def spread_bias():
            bias_turned = ps.tile([P, N], F32, name="bias_turned", tag="chunk2")
            nc.tensor.transpose(bias_turned[:, 0:P], bias_rows[:], ident[:])
            nc.vector.tensor_copy(out=bias_col[:], in_=bias_turned[:, 0:CHUNKS])
            bias_spread = ps.tile([P, N], F32, name="bias_spread", tag="chunk3")
            for c in range(CHUNKS):
                column = bias_col[:, c : c + 1].to_broadcast([P, P])
                nc.tensor.transpose(bias_spread[:, c * P : (c + 1) * P], column, ident[:])
            nc.scalar.copy(out=bias_all[:], in_=bias_spread[:])

        def views(c, z):
            src = raw[c, z][:].rearrange("p j (g i) -> p g j i", i=4)
            dst = grouped[c, z][:].rearrange("p (g i) j -> p g j i", i=4)
            return dst, src

        def interleave_scalar(c, z):
            dst, src = views(c, z)
            nc.scalar.copy(out=dst, in_=src)

        def interleave_vector(c, z):
            dst, src = views(c, z)
            nc.vector.tensor_copy(out=dst, in_=src)

        def quantise(c, z):
            nc.vector.quantize_mx(
                out=wa_codes[c, z][:].bitcast(FP8X4),
                scales=wa_plane[c, z][:],
                in_=grouped[c, z][:].rearrange("p n j -> p (n j)"),
            )

        b0 = [ps.tile([P, N], F32, name="b0_%d" % i, tag="tile%d" % i) for i in range(TILES)]

        def b_product(i):
            cols = slice(i * P, (i + 1) * P)
            for z in range(PASSES):
                nc.tensor.matmul_mx(
                    out=b0[i][:],
                    lhsT=xt[:, z, cols].bitcast(FP8X4),
                    lhsT_scale=xt_plane[:, z, cols],
                    rhs=wc[:, z, :].bitcast(FP4X4),
                    rhs_scale=wc_plane[:, z, :],
                    start=(z == 0),
                    stop=(z == PASSES - 1),
                )

        def b_bias(i):
            nc.vector.tensor_tensor(out=b[i][:], in0=b0[i][:], in1=bias_all[:], op=ALU.add)

        def b_square(i):
            nc.scalar.activation(out=squares[i][:], in_=b[i][:], func=ACT.Square, accum_out=sum_bb[:, i : i + 1])

        a0_t = {}
        passes_done = {c: 0 for c in range(CHUNKS)}

        def flags(c):
            if c not in a0_t:
                a0_t[c] = ps.tile([P, T], F32, name="a0_t%d" % c, tag="chunk%d" % c)
            passes_done[c] = passes_done[c] + 1
            return passes_done[c] == 1, passes_done[c] == PASSES + 1

        def a_second(c):
            cols = slice(c * P, (c + 1) * P)
            start, stop = flags(c)
            nc.tensor.matmul_mx(
                out=a0_t[c][:],
                lhsT=ws[:, cols].bitcast(FP8X4),
                lhsT_scale=ws_plane[:, 0, cols],
                rhs=xq[:].bitcast(FP4X4),
                rhs_scale=xq_plane[:, 0, :],
                start=start,
                stop=stop,
            )

        def a_first(c, z):
            start, stop = flags(c)
            nc.tensor.matmul_mx(
                out=a0_t[c][:],
                lhsT=wa_codes[c, z][:].bitcast(FP8X4),
                lhsT_scale=wa_plane[c, z][:],
                rhs=xt[:, z, :].bitcast(FP8X4),
                rhs_scale=xt_plane[:, z, :],
                start=start,
                stop=stop,
            )

        def a_bias(c):
            nc.scalar.activation(out=a_t[c][:], in_=a0_t[c][:], func=ACT.Identity, bias=bias_col[:, c : c + 1])

        a = {}

        def a_turn(c):
            for i in range(TILES):
                if i not in a:
                    a[i] = ps.tile([P, N], F32, name="a%d" % i, tag="tile%d" % i)
                nc.tensor.transpose(a[i][:, c * P : (c + 1) * P], a_t[c][:, i * P : (i + 1) * P], ident[:])

        def ab_sum(i, h):
            cols = slice(h * N // 2, (h + 1) * N // 2)
            nc.vector.scalar_tensor_tensor(
                out=products[i][:, cols], in0=a[i][:, cols], scalar=1.0, in1=b[i][:, cols],
                op0=ALU.mult, op1=ALU.mult, accum_out=sum_ab[:, i, h : h + 1],
            )

        def denominator():
            nc.vector.tensor_scalar(
                out=neg_den[:], in0=sum_bb[:], scalar1=0.1 * N, scalar2=-1.0, op0=ALU.add, op1=ALU.mult
            )

        def inverse():
            nc.vector.reciprocal(out=neg_inv[:], in_=neg_den[:])

        def coefficient(i):
            nc.vector.tensor_scalar(
                out=neg_coef[:, i : i + 1], in0=sum_ab[:, i, 0:1], scalar1=sum_ab[:, i, 1:2],
                scalar2=neg_inv[:, i : i + 1], op0=ALU.add, op1=ALU.mult,
            )

        def result(i):
            nc.vector.scalar_tensor_tensor(
                out=y[i][:], in0=b[i][:], scalar=neg_coef[:, i : i + 1], in1=a[i][:], op0=ALU.mult, op1=ALU.add
            )
            nc.sync.dma_start(out=out[i * P : (i + 1) * P, :], in_=y[i][:])

        interleave_vector(0, 0)
        spread_bias()
        quantise(0, 0)
        a_first(0, 0)
        for i in range(TILES):
            b_product(i)
        interleave_vector(0, 1)
        interleave_scalar(1, 0)
        interleave_scalar(1, 1)
        quantise(0, 1)
        b_bias(0)
        quantise(1, 0)
        b_bias(1)
        quantise(1, 1)
        b_bias(2)
        b_bias(3)
        a_first(0, 1)
        a_second(0)
        a_first(1, 0)
        a_first(1, 1)
        a_second(1)
        a_second(2)
        a_second(3)
        b_square(0)
        interleave_scalar(2, 0)
        a_bias(0)
        a_bias(1)
        interleave_vector(2, 1)
        quantise(2, 0)
        interleave_vector(3, 0)
        quantise(2, 1)
        interleave_vector(3, 1)
        quantise(3, 0)
        quantise(3, 1)
        a_first(2, 0)
        a_turn(0)
        a_first(2, 1)
        a_turn(1)
        a_first(3, 0)
        a_first(3, 1)
        b_square(1)
        a_bias(2)
        b_square(2)
        a_bias(3)
        b_square(3)
        for i in range(TILES):
            ab_sum(i, 0)
        a_turn(2)
        a_turn(3)
        ab_sum(0, 1)
        denominator()
        ab_sum(1, 1)
        inverse()
        ab_sum(2, 1)
        coefficient(0)
        coefficient(1)
        ab_sum(3, 1)
        coefficient(2)
        result(0)
        coefficient(3)
        result(1)
        result(2)
        result(3)
